import numpy as np
import ml_dtypes


def mxq(x, axis, fmt="e4m3"):
    dtype, down = {"e4m3": (ml_dtypes.float8_e4m3fn, 7), "e5m2": (ml_dtypes.float8_e5m2, 14)}[fmt]
    v = np.moveaxis(np.asarray(x, np.float32).astype(ml_dtypes.bfloat16).astype(np.float64), axis, -1)
    blocks = v.reshape(v.shape[:-1] + (-1, 32))
    amax = np.abs(blocks).max(-1, keepdims=True)
    byte = np.maximum(np.where(amax > 0, np.frexp(amax)[1] - 1 + 127, 0) - down, 1)
    scale = np.exp2(byte - 127.0)
    codes = (blocks / scale).astype(np.float32).astype(dtype).astype(np.float64)
    return np.moveaxis((codes * scale).reshape(v.shape), -1, axis)


WIDE = False


def mx_kscale(k):
    if not WIDE:
        return np.ones(k)
    levels = np.array([10, -10, 5, -5, 0])
    if k % 512:
        return np.exp2(np.random.permutation(np.resize(levels, k // 32))).repeat(32)
    a = np.empty((k // 512, 16))
    for p in range(k // 512):
        a[p, :8] = np.random.permutation(np.resize(levels, 8))
        for g in range(8):
            far = levels[np.abs(levels - a[p, g]) >= 10]
            a[p, g + 8] = far[np.random.randint(len(far))]
    return np.exp2(a.ravel()).repeat(32)


def f64(x):
    return np.asarray(x).astype(np.float64)


def striped(idx):
    return np.tile(idx.reshape(-1, 16).T, (8, 1)).astype(np.uint16)


def unstriped(offs):
    return offs[:16].T.reshape(-1).astype(np.int64)


def pack_weight(w):
    k, n = w.shape
    w = f64(np.asarray(w, np.float32).astype(ml_dtypes.bfloat16)).reshape(k // 32, 32, n)
    amax = np.abs(w).max(1)
    byte = np.clip(np.where(amax > 0, np.frexp(amax)[1] - 1 + 127 - 7, 1), 1, 254)
    scaled = (w * np.exp2(127.0 - byte)[:, None, :]).reshape(k, n).astype(np.float32)
    words = np.ascontiguousarray(scaled.reshape(k // 512, 128, 4, n).transpose(0, 1, 3, 2)).astype(ml_dtypes.float8_e4m3fn).view(np.uint8)
    return words, np.ascontiguousarray(byte.astype(np.uint8).reshape(k // 512, 16, n))


def unpack_weight(words, scales):
    g, p, n, _ = words.shape
    vals = np.ascontiguousarray(words).view(ml_dtypes.float8_e4m3fn).astype(np.float64) * np.repeat(np.exp2(scales.astype(np.float64) - 127.0), 8, axis=1)[..., None]
    return vals.transpose(0, 1, 3, 2).reshape(g * 512, n)


def silu(v):
    return v / (1.0 + np.exp(-np.maximum(v, -700.0)))


K, T, D, S, V, R, N = 1024, 2048, 5, 1280, 256, 8, 512


def setup_inputs():
    n = np.random.standard_normal
    s = mx_kscale(K)[:, None]
    packed = pack_weight(n((K, T)) * s)
    return {
        "x_words": packed[0],
        "x_scales": packed[1],
        "w": (n((D, K, N)) / np.sqrt(D * K) / s[None]).astype(np.float32),
        "b": (0.3 * n((N, 1))).astype(np.float32),
        "offs": striped(np.concatenate([R * np.arange(V) + np.random.randint(0, R, V) for _ in range(D)])),
    }


def reference(x_words, x_scales, w, b, offs):
    idx = unstriped(offs)
    xq = unpack_weight(x_words, x_scales)[:, idx]
    wq = mxq(f64(w), 1, "e4m3")
    y = sum(wq[d].T @ xq[:, d * V:(d + 1) * V] for d in range(D))
    y = silu(y + f64(b))
    return y

@@ -1,0 +1,139 @@
+from contextlib import ExitStack
+
+import concourse.mybir as mybir
+
+K, T, D, V, N = 1024, 2048, 5, 256, 512
+FLOPS = 2 * D * K * N * V
+
+F32 = mybir.dt.float32
+BF16 = mybir.dt.bfloat16
+I32 = mybir.dt.int32
+U32 = mybir.dt.uint32
+U16 = mybir.dt.uint16
+U8 = mybir.dt.uint8
+FP8X4 = mybir.dt.float8_e4m3fn_x4
+SILU = mybir.ActivationFunctionType.Silu
+
+P = 128
+PACK = 4
+K_PASS = P * PACK
+HALVES = K // K_PASS
+M_TILES = N // P
+LIST_COLS = V // 16
+SCALAR_COLS = 320
+
+
+def interleave(copy, dst, src):
+    copy(out=dst.rearrange("p (c i) j -> p c j i", i=4), in_=src.rearrange("p j (c i) -> p c j i", i=4))
+
+
+def tile_picked_deform_lin_silu_def_p_kernel(tc, x_words, x_scales, w, b, offs, out):
+    nc = tc.nc
+
+    def scalar_copy(out, in_):
+        nc.scalar.copy(out, in_)
+
+    def vector_copy(out, in_):
+        nc.vector.tensor_copy(out, in_)
+
+    with ExitStack() as ctx:
+        keep = ctx.enter_context(tc.tile_pool(name="keep", bufs=1))
+        psum = ctx.enter_context(tc.psum_pool(name="psum", bufs=1))
+
+        offsets = keep.tile([P, D * LIST_COLS], U16, name="offsets")
+        word_table = [keep.tile([P, T], U32, name="word_table%d" % o) for o in range(HALVES)]
+        scale_table = keep.tile([P, T], U8, name="scale_table")
+        bias = keep.tile([P, M_TILES], F32, name="bias")
+        warm_in = keep.tile([P, 8], F32, name="warm_in")
+        warm_out = keep.tile([P, 8], F32, name="warm_out")
+
+        nc.vector.memset(scale_table[:].bitcast(I32), 0)
+        for o in range(HALVES):
+            for q in range(4):
+                nc.scalar.dma_start(
+                    out=scale_table[32 * q + 4 * o : 32 * q + 4 * o + 4, :].bitcast(I32),
+                    in_=x_scales[o, 4 * q : 4 * q + 4, :].bitcast(I32),
+                )
+
+        nc.vector.memset(warm_in[:], 0.0)
+        nc.scalar.activation(warm_out[:], warm_in[:], SILU)
+
+        def load_words(o):
+            nc.sync.dma_start(
+                out=word_table[o][:].bitcast(I32),
+                in_=x_words[o].rearrange("p c r -> p (c r)").bitcast(I32),
+            )
+
+        load_words(0)
+        nc.sync.dma_start(offsets[:], offs)
+        load_words(1)
+
+        passes = [(o, d) for o in range(HALVES) for d in range(D)]
+        raw = []
+        for n, (o, d) in enumerate(passes):
+            tile = keep.tile([P, PACK, N], F32, name="raw%d" % n)
+            nc.sync.dma_start(
+                out=tile[:],
+                in_=w[d, o * K_PASS : (o + 1) * K_PASS, :].rearrange("(p j) n -> p j n", j=PACK),
+            )
+            raw.append(tile)
+        with nc.allow_non_contiguous_dma(reason="one bias value a partition and output tile"):
+            nc.sync.dma_start(out=bias[:], in_=b.rearrange("(t p) one -> p (t one)", p=P))
+
+        x_codes = {}
+        x_bytes = {}
+
+        def gather_words(o, d):
+            tile = keep.tile([P, V], U32, name="x_codes%d_%d" % (o, d), align_bytes=64)
+            nc.vector.tensor_copy(tile[:], word_table[o][:].indirect(offsets[:, d * LIST_COLS : (d + 1) * LIST_COLS]))
+            x_codes[(o, d)] = tile
+
+        def gather_bytes(d):
+            tile = keep.tile([P, V], U8, name="x_bytes%d" % d, align_bytes=64)
+            nc.vector.tensor_copy(tile[:], scale_table[:].indirect(offsets[:, d * LIST_COLS : (d + 1) * LIST_COLS]))
+            x_bytes[d] = tile
+
+        for d in range(D):
+            gather_words(0, d)
+        for d in range(D):
+            gather_bytes(d)
+        for d in range(D):
+            gather_words(1, d)
+
+        acc = [psum.tile([P, V], F32, name="acc%d" % m) for m in range(M_TILES)]
+
+        def multiply(n, m, codes, scales):
+            o, d = passes[n]
+            nc.tensor.matmul_mx(
+                out=acc[m][:],
+                lhsT=codes.bitcast(FP8X4),
+                lhsT_scale=scales,
+                rhs=x_codes[(o, d)][:].bitcast(FP8X4),
+                rhs_scale=x_bytes[d][4 * o : P, :],
+                start=(n == 0),
+                stop=(n == len(passes) - 1),
+            )
+
+        last = len(passes) - 1
+        for n in range(last):
+            grouped = keep.tile([P, N, PACK], BF16, name="grouped%d" % n, align_bytes=64)
+            interleave(scalar_copy, grouped[:, :SCALAR_COLS, :], raw[n][:, :, :SCALAR_COLS])
+            interleave(vector_copy, grouped[:, SCALAR_COLS:, :], raw[n][:, :, SCALAR_COLS:])
+            codes = keep.tile([P, N], U32, name="w_codes%d" % n, align_bytes=64)
+            scales = keep.tile([P, N], U8, name="w_scales%d" % n, align_bytes=64)
+            nc.vector.quantize_mx(codes[:].bitcast(FP8X4), scales[:], grouped[:].rearrange("p n j -> p (n j)"))
+            for m in range(M_TILES):
+                multiply(n, m, codes[:, m * P : (m + 1) * P], scales[:, m * P : (m + 1) * P])
+
+        tail = [keep.tile([P, P, PACK], BF16, name="tail%d" % m, align_bytes=64) for m in range(M_TILES)]
+        for m, copy in enumerate((vector_copy, vector_copy, scalar_copy, scalar_copy)):
+            interleave(copy, tail[m][:], raw[last][:, :, m * P : (m + 1) * P])
+        for m in range(M_TILES):
+            codes = keep.tile([P, P], U32, name="tail_codes%d" % m, align_bytes=64)
+            scales = keep.tile([P, P], U8, name="tail_scales%d" % m, align_bytes=64)
+            nc.vector.quantize_mx(codes[:].bitcast(FP8X4), scales[:], tail[m][:].rearrange("p n j -> p (n j)"))
+            multiply(last, m, codes[:], scales[:])
+        for m in range(M_TILES):
+            result = keep.tile([P, V], F32, name="result%d" % m)
+            nc.scalar.activation(result[:], acc[m][:], SILU, bias=bias[:, m : m + 1])
+            nc.sync.dma_start(out=out[m * P : (m + 1) * P, :], in_=result[:])

@@ -1,6 +1,7 @@
 from contextlib import ExitStack
 
 import concourse.mybir as mybir
+from concourse.masks import make_identity
 
 K, T, D, V, N = 1024, 2048, 5, 256, 512
 FLOPS = 2 * D * K * N * V
@@ -47,16 +48,24 @@ def tile_picked_deform_lin_silu_def_p_kernel(tc, x_words, x_scales, w, b, offs, 
         warm_in = keep.tile([P, 8], F32, name="warm_in")
         warm_out = keep.tile([P, 8], F32, name="warm_out")
 
-        nc.vector.memset(scale_table[:].bitcast(I32), 0)
-        for o in range(HALVES):
-            for q in range(4):
-                nc.scalar.dma_start(
-                    out=scale_table[32 * q + 4 * o : 32 * q + 4 * o + 4, :].bitcast(I32),
-                    in_=x_scales[o, 4 * q : 4 * q + 4, :].bitcast(I32),
-                )
+        bias_rows = keep.tile([P, P], F32, name="bias_rows")
+        identity = keep.tile([P, P], F32, name="identity")
+        nc.vector.memset(bias_rows[:], 0.0)
+        nc.scalar.dma_start(out=bias_rows[:M_TILES, :], in_=b.rearrange("(t p) one -> t (p one)", p=P))
 
         nc.vector.memset(warm_in[:], 0.0)
         nc.scalar.activation(warm_out[:], warm_in[:], SILU)
+
+        nc.gpsimd.memset(scale_table[:].bitcast(I32), 0)
+        for q in range(4):
+            nc.gpsimd.dma_start(
+                out=scale_table[32 * q : 32 * q + 4 * HALVES, :].bitcast(I32),
+                in_=x_scales[:, 4 * q : 4 * q + 4, :].bitcast(I32),
+            )
+        make_identity(nc, identity[:])
+        bias_turned = psum.tile([P, P], F32, name="bias_turned")
+        nc.tensor.transpose(bias_turned[:], bias_rows[:], identity[:])
+        nc.scalar.copy(bias[:], bias_turned[:, :M_TILES])
 
         def load_words(o):
             nc.sync.dma_start(
@@ -77,8 +86,6 @@ def tile_picked_deform_lin_silu_def_p_kernel(tc, x_words, x_scales, w, b, offs, 
                 in_=w[d, o * K_PASS : (o + 1) * K_PASS, :].rearrange("(p j) n -> p j n", j=PACK),
             )
             raw.append(tile)
-        with nc.allow_non_contiguous_dma(reason="one bias value a partition and output tile"):
-            nc.sync.dma_start(out=bias[:], in_=b.rearrange("(t p) one -> p (t one)", p=P))
 
         x_codes = {}
         x_bytes = {}

@@ -20,8 +20,9 @@ PACK = 4
 K_PASS = P * PACK
 HALVES = K // K_PASS
 M_TILES = N // P
-LIST_COLS = V // 16
-SCALAR_COLS = 320
+S = D * V
+SCALAR_COLS = 352
+SCALAR_COLS_LATE = 256
 
 
 def interleave(copy, dst, src):
@@ -41,7 +42,7 @@ def tile_picked_deform_lin_silu_def_p_kernel(tc, x_words, x_scales, w, b, offs, 
         keep = ctx.enter_context(tc.tile_pool(name="keep", bufs=1))
         psum = ctx.enter_context(tc.psum_pool(name="psum", bufs=1))
 
-        offsets = keep.tile([P, D * LIST_COLS], U16, name="offsets")
+        offsets = keep.tile([P, S // 16], U16, name="offsets")
         word_table = [keep.tile([P, T], U32, name="word_table%d" % o) for o in range(HALVES)]
         scale_table = keep.tile([P, T], U8, name="scale_table")
         bias = keep.tile([P, M_TILES], F32, name="bias")
@@ -87,25 +88,11 @@ def tile_picked_deform_lin_silu_def_p_kernel(tc, x_words, x_scales, w, b, offs, 
             )
             raw.append(tile)
 
-        x_codes = {}
-        x_bytes = {}
-
-        def gather_words(o, d):
-            tile = keep.tile([P, V], U32, name="x_codes%d_%d" % (o, d), align_bytes=64)
-            nc.vector.tensor_copy(tile[:], word_table[o][:].indirect(offsets[:, d * LIST_COLS : (d + 1) * LIST_COLS]))
-            x_codes[(o, d)] = tile
-
-        def gather_bytes(d):
-            tile = keep.tile([P, V], U8, name="x_bytes%d" % d, align_bytes=64)
-            nc.vector.tensor_copy(tile[:], scale_table[:].indirect(offsets[:, d * LIST_COLS : (d + 1) * LIST_COLS]))
-            x_bytes[d] = tile
-
-        for d in range(D):
-            gather_words(0, d)
-        for d in range(D):
-            gather_bytes(d)
-        for d in range(D):
-            gather_words(1, d)
+        x_codes = [keep.tile([P, S], U32, name="x_codes%d" % o, align_bytes=64) for o in range(HALVES)]
+        x_bytes = keep.tile([P, S], U8, name="x_bytes", align_bytes=64)
+        for o in range(HALVES):
+            nc.vector.tensor_copy(x_codes[o][:], word_table[o][:].indirect(offsets[:]))
+        nc.vector.tensor_copy(x_bytes[:], scale_table[:].indirect(offsets[:]))
 
         acc = [psum.tile([P, V], F32, name="acc%d" % m) for m in range(M_TILES)]
 
@@ -115,8 +102,8 @@ def tile_picked_deform_lin_silu_def_p_kernel(tc, x_words, x_scales, w, b, offs, 
                 out=acc[m][:],
                 lhsT=codes.bitcast(FP8X4),
                 lhsT_scale=scales,
-                rhs=x_codes[(o, d)][:].bitcast(FP8X4),
-                rhs_scale=x_bytes[d][4 * o : P, :],
+                rhs=x_codes[o][:, d * V : (d + 1) * V].bitcast(FP8X4),
+                rhs_scale=x_bytes[4 * o : P, d * V : (d + 1) * V],
                 start=(n == 0),
                 stop=(n == len(passes) - 1),
             )
@@ -124,8 +111,9 @@ def tile_picked_deform_lin_silu_def_p_kernel(tc, x_words, x_scales, w, b, offs, 
         last = len(passes) - 1
         for n in range(last):
             grouped = keep.tile([P, N, PACK], BF16, name="grouped%d" % n, align_bytes=64)
-            interleave(scalar_copy, grouped[:, :SCALAR_COLS, :], raw[n][:, :, :SCALAR_COLS])
-            interleave(vector_copy, grouped[:, SCALAR_COLS:, :], raw[n][:, :, SCALAR_COLS:])
+            split = SCALAR_COLS if n < last - 1 else SCALAR_COLS_LATE
+            interleave(scalar_copy, grouped[:, :split, :], raw[n][:, :, :split])
+            interleave(vector_copy, grouped[:, split:, :], raw[n][:, :, split:])
             codes = keep.tile([P, N], U32, name="w_codes%d" % n, align_bytes=64)
             scales = keep.tile([P, N], U8, name="w_scales%d" % n, align_bytes=64)
             nc.vector.quantize_mx(codes[:].bitcast(FP8X4), scales[:], grouped[:].rearrange("p n j -> p (n j)"))

@@ -46,16 +46,13 @@ def tile_picked_deform_lin_silu_def_p_kernel(tc, x_words, x_scales, w, b, offs, 
         word_table = [keep.tile([P, T], U32, name="word_table%d" % o) for o in range(HALVES)]
         scale_table = keep.tile([P, T], U8, name="scale_table")
         bias = keep.tile([P, M_TILES], F32, name="bias")
-        warm_in = keep.tile([P, 8], F32, name="warm_in")
-        warm_out = keep.tile([P, 8], F32, name="warm_out")
+        zeros = keep.tile([P, P], F32, name="zeros")
 
         bias_rows = keep.tile([P, P], F32, name="bias_rows")
         identity = keep.tile([P, P], F32, name="identity")
-        nc.vector.memset(bias_rows[:], 0.0)
+        nc.vector.memset(zeros[:], 0.0)
+        nc.scalar.activation(bias_rows[:], zeros[:], SILU)
         nc.scalar.dma_start(out=bias_rows[:M_TILES, :], in_=b.rearrange("(t p) one -> t (p one)", p=P))
-
-        nc.vector.memset(warm_in[:], 0.0)
-        nc.scalar.activation(warm_out[:], warm_in[:], SILU)
 
         nc.gpsimd.memset(scale_table[:].bitcast(I32), 0)
         for q in range(4):
@@ -79,14 +76,19 @@ def tile_picked_deform_lin_silu_def_p_kernel(tc, x_words, x_scales, w, b, offs, 
         load_words(1)
 
         passes = [(o, d) for o in range(HALVES) for d in range(D)]
-        raw = []
-        for n, (o, d) in enumerate(passes):
-            tile = keep.tile([P, PACK, N], F32, name="raw%d" % n)
+        last = len(passes) - 1
+
+        def load_weights(n, cols, name):
+            o, d = passes[n]
+            tile = keep.tile([P, PACK, cols.stop - cols.start], F32, name=name)
             nc.sync.dma_start(
                 out=tile[:],
-                in_=w[d, o * K_PASS : (o + 1) * K_PASS, :].rearrange("(p j) n -> p j n", j=PACK),
+                in_=w[d, o * K_PASS : (o + 1) * K_PASS, cols].rearrange("(p j) n -> p j n", j=PACK),
             )
-            raw.append(tile)
+            return tile
+
+        raw = [load_weights(n, slice(0, N), "raw%d" % n) for n in range(last)]
+        raw_last = [load_weights(last, slice(h * 2 * P, (h + 1) * 2 * P), "raw_last%d" % h) for h in range(2)]
 
         x_codes = [keep.tile([P, S], U32, name="x_codes%d" % o, align_bytes=64) for o in range(HALVES)]
         x_bytes = keep.tile([P, S], U8, name="x_bytes", align_bytes=64)
@@ -108,7 +110,6 @@ def tile_picked_deform_lin_silu_def_p_kernel(tc, x_words, x_scales, w, b, offs, 
                 stop=(n == len(passes) - 1),
             )
 
-        last = len(passes) - 1
         for n in range(last):
             grouped = keep.tile([P, N, PACK], BF16, name="grouped%d" % n, align_bytes=64)
             split = SCALAR_COLS if n < last - 1 else SCALAR_COLS_LATE
@@ -120,13 +121,13 @@ def tile_picked_deform_lin_silu_def_p_kernel(tc, x_words, x_scales, w, b, offs, 
             for m in range(M_TILES):
                 multiply(n, m, codes[:, m * P : (m + 1) * P], scales[:, m * P : (m + 1) * P])
 
-        tail = [keep.tile([P, P, PACK], BF16, name="tail%d" % m, align_bytes=64) for m in range(M_TILES)]
-        for m, copy in enumerate((vector_copy, vector_copy, scalar_copy, scalar_copy)):
-            interleave(copy, tail[m][:], raw[last][:, :, m * P : (m + 1) * P])
         for m in range(M_TILES):
+            grouped = keep.tile([P, P, PACK], BF16, name="tail%d" % m, align_bytes=64)
+            copy = (vector_copy, scalar_copy)[m % 2]
+            interleave(copy, grouped[:], raw_last[m // 2][:, :, (m % 2) * P : (m % 2 + 1) * P])
             codes = keep.tile([P, P], U32, name="tail_codes%d" % m, align_bytes=64)
             scales = keep.tile([P, P], U8, name="tail_scales%d" % m, align_bytes=64)
-            nc.vector.quantize_mx(codes[:].bitcast(FP8X4), scales[:], tail[m][:].rearrange("p n j -> p (n j)"))
+            nc.vector.quantize_mx(codes[:].bitcast(FP8X4), scales[:], grouped[:].rearrange("p n j -> p (n j)"))
             multiply(last, m, codes[:], scales[:])
         for m in range(M_TILES):
             result = keep.tile([P, V], F32, name="result%d" % m)

from contextlib import ExitStack

import concourse.mybir as mybir
from concourse.masks import make_identity

K, T, D, V, N = 1024, 2048, 5, 256, 512
FLOPS = 2 * D * K * N * V

F32 = mybir.dt.float32
BF16 = mybir.dt.bfloat16
I32 = mybir.dt.int32
U32 = mybir.dt.uint32
U16 = mybir.dt.uint16
U8 = mybir.dt.uint8
FP8X4 = mybir.dt.float8_e4m3fn_x4
SILU = mybir.ActivationFunctionType.Silu

P = 128
PACK = 4
K_PASS = P * PACK
HALVES = K // K_PASS
M_TILES = N // P
S = D * V
SCALAR_COLS = 352
SCALAR_COLS_LATE = 256


def interleave(copy, dst, src):
    copy(out=dst.rearrange("p (c i) j -> p c j i", i=4), in_=src.rearrange("p j (c i) -> p c j i", i=4))


def tile_picked_deform_lin_silu_def_p_kernel(tc, x_words, x_scales, w, b, offs, out):
    nc = tc.nc

    def scalar_copy(out, in_):
        nc.scalar.copy(out, in_)

    def vector_copy(out, in_):
        nc.vector.tensor_copy(out, in_)

    with ExitStack() as ctx:
        keep = ctx.enter_context(tc.tile_pool(name="keep", bufs=1))
        psum = ctx.enter_context(tc.psum_pool(name="psum", bufs=1))

        offsets = keep.tile([P, S // 16], U16, name="offsets")
        word_table = [keep.tile([P, T], U32, name="word_table%d" % o) for o in range(HALVES)]
        scale_table = keep.tile([P, T], U8, name="scale_table")
        bias = keep.tile([P, M_TILES], F32, name="bias")
        zeros = keep.tile([P, P], F32, name="zeros")

        bias_rows = keep.tile([P, P], F32, name="bias_rows")
        identity = keep.tile([P, P], F32, name="identity")
        nc.vector.memset(zeros[:], 0.0)
        nc.scalar.activation(bias_rows[:], zeros[:], SILU)
        nc.scalar.dma_start(out=bias_rows[:M_TILES, :], in_=b.rearrange("(t p) one -> t (p one)", p=P))

        nc.gpsimd.memset(scale_table[:].bitcast(I32), 0)
        for q in range(4):
            nc.gpsimd.dma_start(
                out=scale_table[32 * q : 32 * q + 4 * HALVES, :].bitcast(I32),
                in_=x_scales[:, 4 * q : 4 * q + 4, :].bitcast(I32),
            )
        make_identity(nc, identity[:])
        bias_turned = psum.tile([P, P], F32, name="bias_turned")
        nc.tensor.transpose(bias_turned[:], bias_rows[:], identity[:])
        nc.scalar.copy(bias[:], bias_turned[:, :M_TILES])

        def load_words(o):
            nc.sync.dma_start(
                out=word_table[o][:].bitcast(I32),
                in_=x_words[o].rearrange("p c r -> p (c r)").bitcast(I32),
            )

        load_words(0)
        nc.sync.dma_start(offsets[:], offs)
        load_words(1)

        passes = [(o, d) for o in range(HALVES) for d in range(D)]
        last = len(passes) - 1

        def load_weights(n, cols, name):
            o, d = passes[n]
            tile = keep.tile([P, PACK, cols.stop - cols.start], F32, name=name)
            nc.sync.dma_start(
                out=tile[:],
                in_=w[d, o * K_PASS : (o + 1) * K_PASS, cols].rearrange("(p j) n -> p j n", j=PACK),
            )
            return tile

        raw = [load_weights(n, slice(0, N), "raw%d" % n) for n in range(last)]
        raw_last = [load_weights(last, slice(h * 2 * P, (h + 1) * 2 * P), "raw_last%d" % h) for h in range(2)]

        x_codes = [keep.tile([P, S], U32, name="x_codes%d" % o, align_bytes=64) for o in range(HALVES)]
        x_bytes = keep.tile([P, S], U8, name="x_bytes", align_bytes=64)
        for o in range(HALVES):
            nc.vector.tensor_copy(x_codes[o][:], word_table[o][:].indirect(offsets[:]))
        nc.vector.tensor_copy(x_bytes[:], scale_table[:].indirect(offsets[:]))

        acc = [psum.tile([P, V], F32, name="acc%d" % m) for m in range(M_TILES)]

        def multiply(n, m, codes, scales):
            o, d = passes[n]
            nc.tensor.matmul_mx(
                out=acc[m][:],
                lhsT=codes.bitcast(FP8X4),
                lhsT_scale=scales,
                rhs=x_codes[o][:, d * V : (d + 1) * V].bitcast(FP8X4),
                rhs_scale=x_bytes[4 * o : P, d * V : (d + 1) * V],
                start=(n == 0),
                stop=(n == len(passes) - 1),
            )

        for n in range(last):
            grouped = keep.tile([P, N, PACK], BF16, name="grouped%d" % n, align_bytes=64)
            split = SCALAR_COLS if n < last - 1 else SCALAR_COLS_LATE
            interleave(scalar_copy, grouped[:, :split, :], raw[n][:, :, :split])
            interleave(vector_copy, grouped[:, split:, :], raw[n][:, :, split:])
            codes = keep.tile([P, N], U32, name="w_codes%d" % n, align_bytes=64)
            scales = keep.tile([P, N], U8, name="w_scales%d" % n, align_bytes=64)
            nc.vector.quantize_mx(codes[:].bitcast(FP8X4), scales[:], grouped[:].rearrange("p n j -> p (n j)"))
            for m in range(M_TILES):
                multiply(n, m, codes[:, m * P : (m + 1) * P], scales[:, m * P : (m + 1) * P])

        for m in range(M_TILES):
            grouped = keep.tile([P, P, PACK], BF16, name="tail%d" % m, align_bytes=64)
            copy = (vector_copy, scalar_copy)[m % 2]
            interleave(copy, grouped[:], raw_last[m // 2][:, :, (m % 2) * P : (m % 2 + 1) * P])
            codes = keep.tile([P, P], U32, name="tail_codes%d" % m, align_bytes=64)
            scales = keep.tile([P, P], U8, name="tail_scales%d" % m, align_bytes=64)
            nc.vector.quantize_mx(codes[:].bitcast(FP8X4), scales[:], grouped[:].rearrange("p n j -> p (n j)"))
            multiply(last, m, codes[:], scales[:])
        for m in range(M_TILES):
            result = keep.tile([P, V], F32, name="result%d" % m)
            nc.scalar.activation(result[:], acc[m][:], SILU, bias=bias[:, m : m + 1])
            nc.sync.dma_start(out=out[m * P : (m + 1) * P, :], in_=result[:])
